import numpy as np
import ml_dtypes


def mxq(x, axis, fmt="e4m3"):
    dtype, down = {"e4m3": (ml_dtypes.float8_e4m3fn, 7), "e5m2": (ml_dtypes.float8_e5m2, 14)}[fmt]
    v = np.moveaxis(np.asarray(x, np.float32).astype(ml_dtypes.bfloat16).astype(np.float64), axis, -1)
    blocks = v.reshape(v.shape[:-1] + (-1, 32))
    amax = np.abs(blocks).max(-1, keepdims=True)
    byte = np.maximum(np.where(amax > 0, np.frexp(amax)[1] - 1 + 127, 0) - down, 1)
    scale = np.exp2(byte - 127.0)
    codes = (blocks / scale).astype(np.float32).astype(dtype).astype(np.float64)
    return np.moveaxis((codes * scale).reshape(v.shape), -1, axis)


WIDE = False


def mx_kscale(k):
    if not WIDE:
        return np.ones(k)
    levels = np.array([10, -10, 5, -5, 0])
    if k % 512:
        return np.exp2(np.random.permutation(np.resize(levels, k // 32))).repeat(32)
    a = np.empty((k // 512, 16))
    for p in range(k // 512):
        a[p, :8] = np.random.permutation(np.resize(levels, 8))
        for g in range(8):
            far = levels[np.abs(levels - a[p, g]) >= 10]
            a[p, g + 8] = far[np.random.randint(len(far))]
    return np.exp2(a.ravel()).repeat(32)


def f64(x):
    return np.asarray(x).astype(np.float64)


def striped(idx):
    return np.tile(idx.reshape(-1, 16).T, (8, 1)).astype(np.uint16)


def unstriped(offs):
    return offs[:16].T.reshape(-1).astype(np.int64)


def striped8(idx):
    return np.concatenate([x.reshape(-1, 16).T for x in idx]).astype(np.uint16)


def runs(offs, k):
    lists = np.stack([offs[16 * r : 16 * r + 16].T.reshape(-1) for r in range(8)]).astype(np.int64)
    return lists[np.arange(k) % 512 // 64]


def pack_weight(w):
    k, n = w.shape
    w = f64(np.asarray(w, np.float32).astype(ml_dtypes.bfloat16)).reshape(k // 32, 32, n)
    amax = np.abs(w).max(1)
    byte = np.clip(np.where(amax > 0, np.frexp(amax)[1] - 1 + 127 - 7, 1), 1, 254)
    scaled = (w * np.exp2(127.0 - byte)[:, None, :]).reshape(k, n).astype(np.float32)
    words = np.ascontiguousarray(scaled.reshape(k // 512, 128, 4, n).transpose(0, 1, 3, 2)).astype(ml_dtypes.float8_e4m3fn).view(np.uint8)
    return words, np.ascontiguousarray(byte.astype(np.uint8).reshape(k // 512, 16, n))


def unpack_weight(words, scales):
    g, p, n, _ = words.shape
    vals = np.ascontiguousarray(words).view(ml_dtypes.float8_e4m3fn).astype(np.float64) * np.repeat(np.exp2(scales.astype(np.float64) - 127.0), 8, axis=1)[..., None]
    return vals.transpose(0, 1, 3, 2).reshape(g * 512, n)

def planes(y):
    n, m = y.shape
    v = y.astype(np.float32).astype(ml_dtypes.bfloat16).astype(np.float64).reshape(n // 32, 32, m)
    top = np.abs(v).max(1)
    byte = np.clip(np.where(top > 0, np.frexp(top)[1] - 1 + 127 - 7, 1), 1, 254)
    codes = (v * np.exp2(127.0 - byte)[:, None, :]).reshape(n, m).astype(np.float32).astype(ml_dtypes.float8_e4m3fn).view(np.uint8)
    words = codes.reshape(n // 512, 128, 4, m).transpose(0, 1, 3, 2)
    return np.ascontiguousarray(words), np.ascontiguousarray(byte.astype(np.uint8).reshape(n // 512, 16, m))


K, T, S, G, H = 512, 1024, 512, 2048, 512


def setup_inputs():
    n = np.random.standard_normal
    s = mx_kscale(K)[:, None]
    packed_xT = pack_weight(n((K, T)) * s)
    packed_dT = pack_weight(n((K, G)) / s)
    return {
        "x_words": packed_xT[0],
        "x_scales": packed_xT[1],
        "d_words": packed_dT[0],
        "d_scales": packed_dT[1],
        "gs": (np.random.uniform(0.5, 1.5, (K, 1)) * s).astype(np.float32),
        "offs": striped(np.random.permutation(T)[:S]),
        "k1": striped8(np.random.randint(0, G, (8, H))),
        "n1": striped8(np.stack([np.random.permutation(S) for _ in range(8)])),
        "n2": striped8(np.stack([np.random.permutation(S) for _ in range(8)])),
        "k2": striped8(np.random.randint(0, G, (8, H))),
        "n3": striped8(np.stack([np.random.permutation(S) for _ in range(8)])),
        "n4": striped8(np.stack([np.random.permutation(S) for _ in range(8)])),
    }


def reference(x_words, x_scales, d_words, d_scales, gs, offs, k1, n1, n2, k2, n3, n4):
    d_k2 = unpack_weight(d_words, d_scales)[np.arange(K)[:, None], runs(k2, K)]
    d_k1 = unpack_weight(d_words, d_scales)[np.arange(K)[:, None], runs(k1, K)]
    xq = unpack_weight(x_words, x_scales)[:, unstriped(offs)]
    h = 0.0625 * (d_k1.T @ xq)
    z = f64(gs) * (0.75 * (h[np.arange(H)[:, None], runs(n1, H)] + h[np.arange(H)[:, None], runs(n2, H)]) - h)
    h2 = 0.0625 * ((d_k2.T @ mxq(z, 0, "e4m3")))
    out_0 = np.minimum(np.maximum(h2, h2[np.arange(H)[:, None], runs(n3, H)]), h2[np.arange(H)[:, None], runs(n4, H)])
    return (out_0,) + planes(out_0)

@@ -1,0 +1,185 @@
+from contextlib import ExitStack
+
+import concourse.mybir as mybir
+
+K, T, S, G, H = 512, 1024, 512, 2048, 512
+FLOPS = 2 * 2 * K * H * S
+
+F32 = mybir.dt.float32
+BF16 = mybir.dt.bfloat16
+I32 = mybir.dt.int32
+U32 = mybir.dt.uint32
+U16 = mybir.dt.uint16
+U8 = mybir.dt.uint8
+FP8X4 = mybir.dt.float8_e4m3fn_x4
+ALU = mybir.AluOpType
+COPY = mybir.ActivationFunctionType.Copy
+
+P = 128
+PACK = 4
+HALF = S // 2
+LANES = 16
+BANK = 512
+CHUNK_EDGES = (0, 256, 384, 512)
+
+
+def tile_picked_codelapminmx_none_po_kernel(tc, x_words, x_scales, d_words, d_scales, gs, offs, k1, n1, n2, k2, n3, n4, out_0, out_1, out_2):
+    nc = tc.nc
+    with ExitStack() as ctx:
+        keep = ctx.enter_context(tc.tile_pool(name="keep", bufs=1))
+        shared = ctx.enter_context(tc.tile_pool(name="shared", bufs=1))
+        psum = ctx.enter_context(tc.psum_pool(name="psum", bufs=1))
+
+        def load_list(src, name):
+            lst = keep.tile([P, S // LANES], U16, name=name)
+            nc.sync.dma_start(lst[:], src)
+            return lst
+
+        def load_scales(src, cols, name):
+            win = keep.tile([P, cols], U8, name=name)
+            nc.sync.dma_start(win[:].bitcast(I32), src[0].bitcast(I32).unsqueeze(1).to_broadcast([16, 8, cols // 4]))
+            return win
+
+        k1_l = load_list(k1, "k1_l")
+        ds_win = load_scales(d_scales, G, "ds_win")
+        offs_l = load_list(offs, "offs_l")
+        xs_win = load_scales(x_scales, T, "xs_win")
+        k2_l = load_list(k2, "k2_l")
+        n2_l = load_list(n2, "n2_l")
+        dw_win = keep.tile([P, G], U32, name="dw_win")
+        nc.sync.dma_start(dw_win[:].bitcast(I32), d_words[0].rearrange("p n t -> p (n t)").bitcast(I32))
+        xw_win = shared.tile([P, T], U32, name="xw_win", offset=0)
+        nc.sync.dma_start(xw_win[:].bitcast(I32), x_words[0].rearrange("p n t -> p (n t)").bitcast(I32))
+        n1_l = load_list(n1, "n1_l")
+        n3_l = load_list(n3, "n3_l")
+        n4_l = load_list(n4, "n4_l")
+        gs_t = keep.tile([P, PACK], F32, name="gs_t")
+        nc.gpsimd.dma_start(gs_t[:], gs.rearrange("(p t) o -> p (t o)", t=PACK))
+        g_nb = keep.tile([P, PACK], F32, name="g_nb")
+        g_own = keep.tile([P, PACK], F32, name="g_own")
+        nc.gpsimd.tensor_scalar(g_nb[:], gs_t[:], 0.75 * 0.0625, 0.0, ALU.mult, ALU.add)
+        nc.gpsimd.tensor_scalar(g_own[:], gs_t[:], -0.0625, 0.0, ALU.mult, ALU.add)
+
+        def deal(dealt, picked):
+            nc.vector.tensor_copy(dealt.rearrange("p (t m) -> p m t", t=PACK), picked.rearrange("p (m t) -> p m t", t=PACK))
+
+        def place_rows(plane):
+            for j in range(1, 4):
+                nc.sync.dma_start(plane[j:P:32, :].bitcast(I32), plane[8 * j:P:32, :].bitcast(I32))
+
+        def weight_words(lst, name, picked):
+            nc.vector.tensor_copy(picked[:], dw_win[:].indirect(lst[:]))
+            dealt = keep.tile([P, H], U32, name=name + "_dealt", align_bytes=64)
+            deal(dealt[:], picked[:])
+            return dealt
+
+        def product(bank, w, ws, t, rhs, rhs_scale):
+            cols = slice(P * t, P * (t + 1))
+            nc.tensor.matmul_mx(out=bank, lhsT=w[:, cols].bitcast(FP8X4), lhsT_scale=ws[:, cols],
+                                rhs=rhs.bitcast(FP8X4), rhs_scale=rhs_scale, start=True, stop=True)
+
+        halves = [slice(HALF * h, HALF * (h + 1)) for h in range(2)]
+        chunks = [slice(a, b) for a, b in zip(CHUNK_EDGES, CHUNK_EDGES[1:])]
+        last = len(chunks) - 1
+
+        def width(cols):
+            return cols.stop - cols.start
+
+        def entries(lst, cols):
+            return lst[:, cols.start // LANES:cols.stop // LANES]
+
+        def banks(name, cols):
+            per_bank = BANK // width(cols)
+            tiles = [psum.tile([P, per_bank, width(cols)], F32, name="%s_%d" % (name, b)) for b in range(PACK // per_bank)]
+            return [tiles[t // per_bank][:, t % per_bank, :] for t in range(PACK)]
+
+        def woven(ap):
+            return ap.rearrange("p (c i) t -> p c t i", i=4)
+
+        def planes(ap):
+            return ap.rearrange("p t (c i) -> p c t i", i=4)
+
+        w1s_picked = keep.tile([P, H], U8, name="w1s_picked")
+        nc.vector.tensor_copy(w1s_picked[:], ds_win[:].indirect(k1_l[:]))
+        xs_picked = keep.tile([P, S], U8, name="xs_picked")
+        nc.vector.tensor_copy(xs_picked[:], xs_win[:].indirect(offs_l[:]))
+        scales1 = keep.tile([P, H + S], U8, name="scales1", align_bytes=64)
+        w1s, xs = scales1[:, :H], scales1[:, H:]
+        deal(w1s, w1s_picked[:])
+        nc.vector.tensor_copy(xs.bitcast(I32), xs_picked[:].bitcast(I32))
+        place_rows(scales1)
+        w1 = weight_words(k1_l, "w1", keep.tile([P, H], U32, name="w1_picked"))
+        nb = [keep.tile([P, S], F32, name="nb%d" % t) for t in range(PACK)]
+        h2 = [keep.tile([P, S], F32, name="h2_%d" % t) for t in range(PACK)]
+        acc1 = []
+        for h, cols in enumerate(halves):
+            xw = keep.tile([P, HALF], U32, name="xw%d" % h, align_bytes=64)
+            nc.vector.tensor_copy(xw[:], xw_win[:].indirect(entries(offs_l, cols)))
+            acc1.append(banks("acc1_%d" % h, cols))
+            for t in range(PACK):
+                product(acc1[h][t], w1, w1s, t, xw[:], xs[:, cols])
+            for t in range(PACK):
+                nc.scalar.activation(nb[t][:, cols], acc1[h][t], COPY, scale=g_nb[:, t:t + 1])
+
+        w2s_picked = shared.tile([P, H], U8, name="w2s_picked", offset=0)
+        nc.vector.tensor_copy(w2s_picked[:], ds_win[:].indirect(k2_l[:]))
+        w2s = keep.tile([P, H], U8, name="w2s", align_bytes=64)
+        deal(w2s[:], w2s_picked[:])
+        place_rows(w2s)
+        w2 = weight_words(k2_l, "w2", shared.tile([P, H], U32, name="w2_picked", offset=H))
+
+        own = keep.tile([P, PACK, S], F32, name="own")
+        acc2 = []
+        for c, cols in enumerate(chunks):
+            n = width(cols)
+            if cols.start % HALF == 0:
+                h = cols.start // HALF
+                for t in range(PACK):
+                    nc.scalar.activation(own[:, t, halves[h]], acc1[h][t], COPY, scale=g_own[:, t:t + 1])
+            first = keep.tile([P, PACK, n], F32, name="first%d" % c)
+            rest = keep.tile([P, PACK, n], F32, name="rest%d" % c)
+            for t in range(PACK):
+                nc.vector.tensor_tensor(rest[:, t, :], nb[t][:].indirect(entries(n2_l, cols)), own[:, t, cols], ALU.add)
+                nc.scalar.activation(first[:, t, :], nb[t][:].indirect(entries(n1_l, cols)), COPY)
+            z = keep.tile([P, n, PACK], BF16, name="z%d" % c, align_bytes=64)
+            nc.vector.tensor_tensor(woven(z[:]), planes(first[:]), planes(rest[:]), ALU.add)
+            zw = keep.tile([P, n], U32, name="zw%d" % c, align_bytes=64)
+            zs = keep.tile([P, n], U8, name="zs%d" % c, align_bytes=64)
+            nc.vector.quantize_mx(out=zw[:].bitcast(FP8X4), scales=zs[:], in_=z[:].rearrange("p c t -> p (c t)"))
+            acc2.append(banks("acc2_%d" % c, cols))
+            for t in range(PACK):
+                product(acc2[c][t], w2, w2s, t, zw[:], zs[:])
+        for c in range(last):
+            for t in range(PACK):
+                nc.scalar.activation(h2[t][:, chunks[c]], acc2[c][t], COPY, scale=0.0625)
+
+        out_rows = out_0.rearrange("(p t) s -> p t s", t=PACK)
+        words_out = out_1[0].rearrange("p n t -> p (n t)").bitcast(I32)
+        ys = keep.tile([P, S], U8, name="ys", align_bytes=64)
+        for c, cols in enumerate(chunks):
+            n = width(cols)
+            y = keep.tile([P, PACK, n], F32, name="y%d" % c)
+            third = keep.tile([P, PACK, n], F32, name="third%d" % c)
+            fourth = keep.tile([P, PACK, n], F32, name="fourth%d" % c)
+            upper = keep.tile([P, PACK, n], F32, name="upper%d" % c)
+            for t in range(PACK + 1):
+                if t < PACK:
+                    if c == 0:
+                        nc.scalar.activation(h2[t][:, chunks[last]], acc2[last][t], COPY, scale=0.0625)
+                    nc.scalar.activation(third[:, t, :], h2[t][:].indirect(entries(n3_l, cols)), COPY)
+                    if c == 0 and t < 4:
+                        nc.vector.tensor_copy(fourth[:, t, :], h2[t][:].indirect(entries(n4_l, cols)))
+                    else:
+                        nc.scalar.activation(fourth[:, t, :], h2[t][:].indirect(entries(n4_l, cols)), COPY)
+                    nc.vector.tensor_tensor(upper[:, t, :], h2[t][:, cols], third[:, t, :], ALU.max)
+                if t > 0:
+                    nc.vector.tensor_tensor(y[:, t - 1, :], upper[:, t - 1, :], fourth[:, t - 1, :], ALU.min)
+            nc.sync.dma_start(out_rows[:, :, cols], y[:])
+            yb = keep.tile([P, n, PACK], BF16, name="yb%d" % c, align_bytes=64)
+            nc.vector.tensor_copy(woven(yb[:]), planes(y[:]))
+            yw = keep.tile([P, n], U32, name="yw%d" % c, align_bytes=64)
+            nc.vector.quantize_mx(out=yw[:].bitcast(FP8X4), scales=ys[:, cols], in_=yb[:].rearrange("p c t -> p (c t)"))
+            nc.sync.dma_start(words_out[:, cols], yw[:].bitcast(I32))
+        for q in range(4):
+            queue = nc.sync if q % 2 == 0 else nc.scalar
+            queue.dma_start(out_2[0, 4 * q:4 * q + 4, :].bitcast(I32), ys[32 * q:32 * q + 4, :].bitcast(I32))

@@ -19,7 +19,10 @@ P = 128
 PACK = 4
 HALF = S // 2
 LANES = 16
-BANK = 512
+PAIRS = (range(0, 2), range(2, 4))
+GROUPS = (PAIRS, (range(0, 4),), (range(0, 1), range(1, 4)))
+TAGS = (("b4", "b5"), ("b6",), ("b7", "b0"))
+ON_VECTOR = (4, 1, 0)
 CHUNK_EDGES = (0, 256, 384, 512)
 
 
@@ -40,25 +43,25 @@ def tile_picked_codelapminmx_none_po_kernel(tc, x_words, x_scales, d_words, d_sc
             nc.sync.dma_start(win[:].bitcast(I32), src[0].bitcast(I32).unsqueeze(1).to_broadcast([16, 8, cols // 4]))
             return win
 
-        k1_l = load_list(k1, "k1_l")
-        ds_win = load_scales(d_scales, G, "ds_win")
         offs_l = load_list(offs, "offs_l")
         xs_win = load_scales(x_scales, T, "xs_win")
+        k1_l = load_list(k1, "k1_l")
+        ds_win = load_scales(d_scales, G, "ds_win")
+        gs_t = keep.tile([P, PACK], F32, name="gs_t")
+        nc.sync.dma_start(gs_t[:], gs.rearrange("(p t) o -> p (t o)", t=PACK))
         k2_l = load_list(k2, "k2_l")
-        n2_l = load_list(n2, "n2_l")
         dw_win = keep.tile([P, G], U32, name="dw_win")
         nc.sync.dma_start(dw_win[:].bitcast(I32), d_words[0].rearrange("p n t -> p (n t)").bitcast(I32))
         xw_win = shared.tile([P, T], U32, name="xw_win", offset=0)
         nc.sync.dma_start(xw_win[:].bitcast(I32), x_words[0].rearrange("p n t -> p (n t)").bitcast(I32))
+        n2_l = load_list(n2, "n2_l")
         n1_l = load_list(n1, "n1_l")
         n3_l = load_list(n3, "n3_l")
         n4_l = load_list(n4, "n4_l")
-        gs_t = keep.tile([P, PACK], F32, name="gs_t")
-        nc.gpsimd.dma_start(gs_t[:], gs.rearrange("(p t) o -> p (t o)", t=PACK))
         g_nb = keep.tile([P, PACK], F32, name="g_nb")
         g_own = keep.tile([P, PACK], F32, name="g_own")
-        nc.gpsimd.tensor_scalar(g_nb[:], gs_t[:], 0.75 * 0.0625, 0.0, ALU.mult, ALU.add)
-        nc.gpsimd.tensor_scalar(g_own[:], gs_t[:], -0.0625, 0.0, ALU.mult, ALU.add)
+        nc.scalar.activation(g_nb[:], gs_t[:], COPY, scale=0.75 * 0.0625)
+        nc.scalar.activation(g_own[:], gs_t[:], COPY, scale=-0.0625)
 
         def deal(dealt, picked):
             nc.vector.tensor_copy(dealt.rearrange("p (t m) -> p m t", t=PACK), picked.rearrange("p (m t) -> p m t", t=PACK))
@@ -88,10 +91,9 @@ def tile_picked_codelapminmx_none_po_kernel(tc, x_words, x_scales, d_words, d_sc
         def entries(lst, cols):
             return lst[:, cols.start // LANES:cols.stop // LANES]
 
-        def banks(name, cols):
-            per_bank = BANK // width(cols)
-            tiles = [psum.tile([P, per_bank, width(cols)], F32, name="%s_%d" % (name, b)) for b in range(PACK // per_bank)]
-            return [tiles[t // per_bank][:, t % per_bank, :] for t in range(PACK)]
+        def banks(name, cols, groups, tags):
+            tiles = [psum.tile([P, len(g), width(cols)], F32, name="%s_%d" % (name, b), tag=tags[b]) for b, g in enumerate(groups)]
+            return tiles, [tiles[b][:, i, :] for b, g in enumerate(groups) for i in range(len(g))]
 
         def woven(ap):
             return ap.rearrange("p (c i) t -> p c t i", i=4)
@@ -99,10 +101,10 @@ def tile_picked_codelapminmx_none_po_kernel(tc, x_words, x_scales, d_words, d_sc
         def planes(ap):
             return ap.rearrange("p t (c i) -> p c t i", i=4)
 
-        w1s_picked = keep.tile([P, H], U8, name="w1s_picked")
-        nc.vector.tensor_copy(w1s_picked[:], ds_win[:].indirect(k1_l[:]))
         xs_picked = keep.tile([P, S], U8, name="xs_picked")
         nc.vector.tensor_copy(xs_picked[:], xs_win[:].indirect(offs_l[:]))
+        w1s_picked = keep.tile([P, H], U8, name="w1s_picked")
+        nc.vector.tensor_copy(w1s_picked[:], ds_win[:].indirect(k1_l[:]))
         scales1 = keep.tile([P, H + S], U8, name="scales1", align_bytes=64)
         w1s, xs = scales1[:, :H], scales1[:, H:]
         deal(w1s, w1s_picked[:])
@@ -115,7 +117,7 @@ def tile_picked_codelapminmx_none_po_kernel(tc, x_words, x_scales, d_words, d_sc
         for h, cols in enumerate(halves):
             xw = keep.tile([P, HALF], U32, name="xw%d" % h, align_bytes=64)
             nc.vector.tensor_copy(xw[:], xw_win[:].indirect(entries(offs_l, cols)))
-            acc1.append(banks("acc1_%d" % h, cols))
+            acc1.append(banks("acc1_%d" % h, cols, PAIRS, ("b%d" % (2 * h), "b%d" % (2 * h + 1)))[1])
             for t in range(PACK):
                 product(acc1[h][t], w1, w1s, t, xw[:], xs[:, cols])
             for t in range(PACK):
@@ -128,28 +130,35 @@ def tile_picked_codelapminmx_none_po_kernel(tc, x_words, x_scales, d_words, d_sc
         place_rows(w2s)
         w2 = weight_words(k2_l, "w2", shared.tile([P, H], U32, name="w2_picked", offset=H))
 
-        own = keep.tile([P, PACK, S], F32, name="own")
+        first = keep.tile([P, PACK, S], F32, name="first")
+        for cols in chunks:
+            for t in range(PACK):
+                nc.scalar.activation(first[:, t, cols], nb[t][:].indirect(entries(n1_l, cols)), COPY)
         acc2 = []
+        bank2 = []
         for c, cols in enumerate(chunks):
             n = width(cols)
-            if cols.start % HALF == 0:
-                h = cols.start // HALF
-                for t in range(PACK):
-                    nc.scalar.activation(own[:, t, halves[h]], acc1[h][t], COPY, scale=g_own[:, t:t + 1])
-            first = keep.tile([P, PACK, n], F32, name="first%d" % c)
-            rest = keep.tile([P, PACK, n], F32, name="rest%d" % c)
-            for t in range(PACK):
-                nc.vector.tensor_tensor(rest[:, t, :], nb[t][:].indirect(entries(n2_l, cols)), own[:, t, cols], ALU.add)
-                nc.scalar.activation(first[:, t, :], nb[t][:].indirect(entries(n1_l, cols)), COPY)
+            h = cols.start // HALF
+            local = slice(cols.start - h * HALF, cols.stop - h * HALF)
+            both = keep.tile([P, PACK, n], F32, name="both%d" % c)
+            zp = keep.tile([P, PACK, n], BF16, name="zp%d" % c)
+            for t in range(PACK + 1):
+                if t < PACK:
+                    nc.vector.tensor_tensor(both[:, t, :], nb[t][:].indirect(entries(n2_l, cols)), first[:, t, cols], ALU.add)
+                if t > 0:
+                    nc.vector.scalar_tensor_tensor(zp[:, t - 1, :], acc1[h][t - 1][:, local], g_own[:, t - 1:t], both[:, t - 1, :], ALU.mult, ALU.add)
             z = keep.tile([P, n, PACK], BF16, name="z%d" % c, align_bytes=64)
-            nc.vector.tensor_tensor(woven(z[:]), planes(first[:]), planes(rest[:]), ALU.add)
+            weave = nc.scalar.copy if c < 2 else nc.vector.tensor_copy
+            weave(woven(z[:]), planes(zp[:]))
             zw = keep.tile([P, n], U32, name="zw%d" % c, align_bytes=64)
             zs = keep.tile([P, n], U8, name="zs%d" % c, align_bytes=64)
             nc.vector.quantize_mx(out=zw[:].bitcast(FP8X4), scales=zs[:], in_=z[:].rearrange("p c t -> p (c t)"))
-            acc2.append(banks("acc2_%d" % c, cols))
+            tiles, sums = banks("acc2_%d" % c, cols, GROUPS[c], TAGS[c])
+            bank2.append(tiles)
+            acc2.append(sums)
             for t in range(PACK):
                 product(acc2[c][t], w2, w2s, t, zw[:], zs[:])
-        for c in range(last):
+        for c in range(len(chunks)):
             for t in range(PACK):
                 nc.scalar.activation(h2[t][:, chunks[c]], acc2[c][t], COPY, scale=0.0625)
 
@@ -162,18 +171,19 @@ def tile_picked_codelapminmx_none_po_kernel(tc, x_words, x_scales, d_words, d_sc
             third = keep.tile([P, PACK, n], F32, name="third%d" % c)
             fourth = keep.tile([P, PACK, n], F32, name="fourth%d" % c)
             upper = keep.tile([P, PACK, n], F32, name="upper%d" % c)
-            for t in range(PACK + 1):
-                if t < PACK:
-                    if c == 0:
-                        nc.scalar.activation(h2[t][:, chunks[last]], acc2[last][t], COPY, scale=0.0625)
-                    nc.scalar.activation(third[:, t, :], h2[t][:].indirect(entries(n3_l, cols)), COPY)
-                    if c == 0 and t < 4:
-                        nc.vector.tensor_copy(fourth[:, t, :], h2[t][:].indirect(entries(n4_l, cols)))
-                    else:
-                        nc.scalar.activation(fourth[:, t, :], h2[t][:].indirect(entries(n4_l, cols)), COPY)
-                    nc.vector.tensor_tensor(upper[:, t, :], h2[t][:, cols], third[:, t, :], ALU.max)
-                if t > 0:
-                    nc.vector.tensor_tensor(y[:, t - 1, :], upper[:, t - 1, :], fourth[:, t - 1, :], ALU.min)
+            for t in range(PACK):
+                if t < ON_VECTOR[c]:
+                    nc.vector.tensor_copy(fourth[:, t, :], h2[t][:].indirect(entries(n4_l, cols)))
+            for t in range(PACK):
+                nc.scalar.activation(third[:, t, :], h2[t][:].indirect(entries(n3_l, cols)), COPY)
+            for t in range(PACK):
+                if t >= ON_VECTOR[c]:
+                    nc.scalar.activation(fourth[:, t, :], h2[t][:].indirect(entries(n4_l, cols)), COPY)
+            for bank, group in zip(bank2[c], GROUPS[c]):
+                rows = slice(group.start, group.stop)
+                nc.vector.scalar_tensor_tensor(upper[:, rows, :], bank[:], 0.0625, third[:, rows, :], ALU.mult, ALU.max)
+            for rows in (slice(0, 3), slice(3, 4)) if c == last else (slice(0, 2), slice(2, 4)):
+                nc.vector.tensor_tensor(y[:, rows, :], upper[:, rows, :], fourth[:, rows, :], ALU.min)
             nc.sync.dma_start(out_rows[:, :, cols], y[:])
             yb = keep.tile([P, n, PACK], BF16, name="yb%d" % c, align_bytes=64)
             nc.vector.tensor_copy(woven(yb[:]), planes(y[:]))

@@ -19,6 +19,7 @@ P = 128
 PACK = 4
 HALF = S // 2
 LANES = 16
+BOTH_ON_SCALAR = 2
 PAIRS = (range(0, 2), range(2, 4))
 GROUPS = (PAIRS, (range(0, 4),), (range(0, 1), range(1, 4)))
 TAGS = (("b4", "b5"), ("b6",), ("b7", "b0"))
@@ -38,15 +39,18 @@ def tile_picked_codelapminmx_none_po_kernel(tc, x_words, x_scales, d_words, d_sc
             nc.sync.dma_start(lst[:], src)
             return lst
 
-        def load_scales(src, cols, name):
-            win = keep.tile([P, cols], U8, name=name)
-            nc.sync.dma_start(win[:].bitcast(I32), src[0].bitcast(I32).unsqueeze(1).to_broadcast([16, 8, cols // 4]))
-            return win
+        def load_scales(src, win):
+            nc.sync.dma_start(win[0:P:8, :].bitcast(I32), src[0].bitcast(I32))
+
+        xs_win = keep.tile([P, T], U8, name="xs_win")
+        ds_win = keep.tile([P, G], U8, name="ds_win")
+        nc.vector.memset(xs_win[:].bitcast(I32), 0)
+        nc.vector.memset(ds_win[:].bitcast(I32), 0)
 
         offs_l = load_list(offs, "offs_l")
-        xs_win = load_scales(x_scales, T, "xs_win")
         k1_l = load_list(k1, "k1_l")
-        ds_win = load_scales(d_scales, G, "ds_win")
+        load_scales(x_scales, xs_win)
+        load_scales(d_scales, ds_win)
         gs_t = keep.tile([P, PACK], F32, name="gs_t")
         nc.sync.dma_start(gs_t[:], gs.rearrange("(p t) o -> p (t o)", t=PACK))
         k2_l = load_list(k2, "k2_l")
@@ -134,6 +138,9 @@ def tile_picked_codelapminmx_none_po_kernel(tc, x_words, x_scales, d_words, d_sc
         for cols in chunks:
             for t in range(PACK):
                 nc.scalar.activation(first[:, t, cols], nb[t][:].indirect(entries(n1_l, cols)), COPY)
+        second = keep.tile([P, BOTH_ON_SCALAR, width(chunks[last])], F32, name="second")
+        for t in range(BOTH_ON_SCALAR):
+            nc.scalar.activation(second[:, t, :], nb[t][:].indirect(entries(n2_l, chunks[last])), COPY)
         acc2 = []
         bank2 = []
         for c, cols in enumerate(chunks):
@@ -143,7 +150,10 @@ def tile_picked_codelapminmx_none_po_kernel(tc, x_words, x_scales, d_words, d_sc
             both = keep.tile([P, PACK, n], F32, name="both%d" % c)
             zp = keep.tile([P, PACK, n], BF16, name="zp%d" % c)
             for t in range(PACK + 1):
-                if t < PACK:
+                if c == last and t < BOTH_ON_SCALAR:
+                    if t == 0:
+                        nc.vector.tensor_tensor(both[:, :BOTH_ON_SCALAR, :], second[:], first[:, :BOTH_ON_SCALAR, cols], ALU.add)
+                elif t < PACK:
                     nc.vector.tensor_tensor(both[:, t, :], nb[t][:].indirect(entries(n2_l, cols)), first[:, t, cols], ALU.add)
                 if t > 0:
                     nc.vector.scalar_tensor_tensor(zp[:, t - 1, :], acc1[h][t - 1][:, local], g_own[:, t - 1:t], both[:, t - 1, :], ALU.mult, ALU.add)

@@ -20,6 +20,7 @@ PACK = 4
 HALF = S // 2
 LANES = 16
 BOTH_ON_SCALAR = 2
+SINGLES = (range(0, 1), range(1, 2), range(2, 3), range(3, 4))
 PAIRS = (range(0, 2), range(2, 4))
 GROUPS = (PAIRS, (range(0, 4),), (range(0, 1), range(1, 4)))
 TAGS = (("b4", "b5"), ("b6",), ("b7", "b0"))
@@ -121,7 +122,7 @@ def tile_picked_codelapminmx_none_po_kernel(tc, x_words, x_scales, d_words, d_sc
         for h, cols in enumerate(halves):
             xw = keep.tile([P, HALF], U32, name="xw%d" % h, align_bytes=64)
             nc.vector.tensor_copy(xw[:], xw_win[:].indirect(entries(offs_l, cols)))
-            acc1.append(banks("acc1_%d" % h, cols, PAIRS, ("b%d" % (2 * h), "b%d" % (2 * h + 1)))[1])
+            acc1.append(banks("acc1_%d" % h, cols, SINGLES, ["b%d" % (PACK * (1 - h) + t) for t in range(PACK)])[1])
             for t in range(PACK):
                 product(acc1[h][t], w1, w1s, t, xw[:], xs[:, cols])
             for t in range(PACK):
@@ -147,6 +148,7 @@ def tile_picked_codelapminmx_none_po_kernel(tc, x_words, x_scales, d_words, d_sc
             n = width(cols)
             h = cols.start // HALF
             local = slice(cols.start - h * HALF, cols.stop - h * HALF)
+            parts = [slice(0, n // 2), slice(n // 2, n)] if c == last else [slice(0, n)]
             both = keep.tile([P, PACK, n], F32, name="both%d" % c)
             zp = keep.tile([P, PACK, n], BF16, name="zp%d" % c)
             for t in range(PACK + 1):
@@ -156,13 +158,17 @@ def tile_picked_codelapminmx_none_po_kernel(tc, x_words, x_scales, d_words, d_sc
                 elif t < PACK:
                     nc.vector.tensor_tensor(both[:, t, :], nb[t][:].indirect(entries(n2_l, cols)), first[:, t, cols], ALU.add)
                 if t > 0:
-                    nc.vector.scalar_tensor_tensor(zp[:, t - 1, :], acc1[h][t - 1][:, local], g_own[:, t - 1:t], both[:, t - 1, :], ALU.mult, ALU.add)
+                    for part in parts if t == PACK else [slice(0, n)]:
+                        nc.vector.scalar_tensor_tensor(zp[:, t - 1, part], acc1[h][t - 1][:, local][:, part], g_own[:, t - 1:t],
+                                                       both[:, t - 1, part], ALU.mult, ALU.add)
             z = keep.tile([P, n, PACK], BF16, name="z%d" % c, align_bytes=64)
-            weave = nc.scalar.copy if c < 2 else nc.vector.tensor_copy
-            weave(woven(z[:]), planes(zp[:]))
+            weave = nc.scalar.copy if c < last else nc.vector.tensor_copy
             zw = keep.tile([P, n], U32, name="zw%d" % c, align_bytes=64)
             zs = keep.tile([P, n], U8, name="zs%d" % c, align_bytes=64)
-            nc.vector.quantize_mx(out=zw[:].bitcast(FP8X4), scales=zs[:], in_=z[:].rearrange("p c t -> p (c t)"))
+            for part in parts:
+                weave(woven(z[:, part, :]), planes(zp[:, :, part]))
+            for part in parts:
+                nc.vector.quantize_mx(out=zw[:, part].bitcast(FP8X4), scales=zs[:, part], in_=z[:, part, :].rearrange("p c t -> p (c t)"))
             tiles, sums = banks("acc2_%d" % c, cols, GROUPS[c], TAGS[c])
             bank2.append(tiles)
             acc2.append(sums)
@@ -192,13 +198,18 @@ def tile_picked_codelapminmx_none_po_kernel(tc, x_words, x_scales, d_words, d_sc
             for bank, group in zip(bank2[c], GROUPS[c]):
                 rows = slice(group.start, group.stop)
                 nc.vector.scalar_tensor_tensor(upper[:, rows, :], bank[:], 0.0625, third[:, rows, :], ALU.mult, ALU.max)
-            for rows in (slice(0, 3), slice(3, 4)) if c == last else (slice(0, 2), slice(2, 4)):
-                nc.vector.tensor_tensor(y[:, rows, :], upper[:, rows, :], fourth[:, rows, :], ALU.min)
+            parts = [slice(0, n // 2), slice(n // 2, n)] if c == last else [slice(0, n)]
+            split = 3 if c == last else 2
+            nc.vector.tensor_tensor(y[:, :split, :], upper[:, :split, :], fourth[:, :split, :], ALU.min)
+            for part in parts:
+                nc.vector.tensor_tensor(y[:, split:, part], upper[:, split:, part], fourth[:, split:, part], ALU.min)
             nc.sync.dma_start(out_rows[:, :, cols], y[:])
             yb = keep.tile([P, n, PACK], BF16, name="yb%d" % c, align_bytes=64)
-            nc.vector.tensor_copy(woven(yb[:]), planes(y[:]))
             yw = keep.tile([P, n], U32, name="yw%d" % c, align_bytes=64)
-            nc.vector.quantize_mx(out=yw[:].bitcast(FP8X4), scales=ys[:, cols], in_=yb[:].rearrange("p c t -> p (c t)"))
+            for part in parts:
+                nc.vector.tensor_copy(woven(yb[:, part, :]), planes(y[:, :, part]))
+            for part in parts:
+                nc.vector.quantize_mx(out=yw[:, part].bitcast(FP8X4), scales=ys[:, cols][:, part], in_=yb[:, part, :].rearrange("p c t -> p (c t)"))
             nc.sync.dma_start(words_out[:, cols], yw[:].bitcast(I32))
         for q in range(4):
             queue = nc.sync if q % 2 == 0 else nc.scalar

@@ -17,23 +17,40 @@ COPY = mybir.ActivationFunctionType.Copy
 
 P = 128
 PACK = 4
-HALF = S // 2
 LANES = 16
-BOTH_ON_SCALAR = 2
+QUADRANT = 32
+BLOCK_PARTITIONS = 8
+SIXTEENTH = 0.0625
+
+HALVES = (slice(0, 256), slice(256, 512))
+CHUNKS = (slice(0, 256), slice(256, 384), slice(384, 512))
+LAST = len(CHUNKS) - 1
 SINGLES = (range(0, 1), range(1, 2), range(2, 3), range(3, 4))
-PAIRS = (range(0, 2), range(2, 4))
-GROUPS = (PAIRS, (range(0, 4),), (range(0, 1), range(1, 4)))
-TAGS = (("b4", "b5"), ("b6",), ("b7", "b0"))
-ON_VECTOR = (4, 1, 0)
-CHUNK_EDGES = (0, 256, 384, 512)
+BANK_GROUPS = ((range(0, 2), range(2, 4)), (range(0, 4),), (range(0, 1), range(1, 4)))
+FIRST_BANKS = (("b4", "b5", "b6", "b7"), ("b0", "b1", "b2", "b3"))
+SECOND_BANKS = (("b4", "b5"), ("b6",), ("b7", "b0"))
+N2_ON_SCALAR = 2
+N4_ON_VECTOR = (4, 1, 0)
 
 
-def tile_picked_codelapminmx_none_po_kernel(tc, x_words, x_scales, d_words, d_scales, gs, offs, k1, n1, n2, k2, n3, n4, out_0, out_1, out_2):
+def tile_picked_codelapminmx_none_po_kernel(
+    tc, x_words, x_scales, d_words, d_scales, gs, offs, k1, n1, n2, k2, n3, n4, out_0, out_1, out_2
+):
     nc = tc.nc
     with ExitStack() as ctx:
         keep = ctx.enter_context(tc.tile_pool(name="keep", bufs=1))
         shared = ctx.enter_context(tc.tile_pool(name="shared", bufs=1))
         psum = ctx.enter_context(tc.psum_pool(name="psum", bufs=1))
+
+        def width(cols):
+            return cols.stop - cols.start
+
+        def entries(lst, cols):
+            return lst[:, cols.start // LANES:cols.stop // LANES]
+
+        def pieces(c):
+            n = width(CHUNKS[c])
+            return [slice(0, n // 2), slice(n // 2, n)] if c == LAST else [slice(0, n)]
 
         def load_list(src, name):
             lst = keep.tile([P, S // LANES], U16, name=name)
@@ -41,13 +58,40 @@ def tile_picked_codelapminmx_none_po_kernel(tc, x_words, x_scales, d_words, d_sc
             return lst
 
         def load_scales(src, win):
-            nc.sync.dma_start(win[0:P:8, :].bitcast(I32), src[0].bitcast(I32))
+            nc.sync.dma_start(win[0:P:BLOCK_PARTITIONS, :].bitcast(I32), src[0].bitcast(I32))
+
+        def deal(dealt, picked):
+            nc.vector.tensor_copy(dealt.rearrange("p (t m) -> p m t", t=PACK), picked.rearrange("p (m t) -> p m t", t=PACK))
+
+        def place_rows(scales, queues):
+            for j, queue in zip(range(1, PACK), queues):
+                queue.dma_start(scales[j:P:QUADRANT, :].bitcast(I32), scales[BLOCK_PARTITIONS * j:P:QUADRANT, :].bitcast(I32))
+
+        def weight_words(lst, name, picked):
+            nc.vector.tensor_copy(picked[:], dw_win[:].indirect(lst[:]))
+            dealt = keep.tile([P, H], U32, name=name, align_bytes=64)
+            deal(dealt[:], picked[:])
+            return dealt
+
+        def banks(name, cols, groups, tags):
+            tiles = [psum.tile([P, len(g), width(cols)], F32, name="%s_%d" % (name, b), tag=tags[b]) for b, g in enumerate(groups)]
+            return tiles, [tiles[b][:, i, :] for b, g in enumerate(groups) for i in range(len(g))]
+
+        def product(sums, w, ws, t, rhs, rhs_scale):
+            cols = slice(P * t, P * (t + 1))
+            nc.tensor.matmul_mx(out=sums, lhsT=w[:, cols].bitcast(FP8X4), lhsT_scale=ws[:, cols],
+                                rhs=rhs.bitcast(FP8X4), rhs_scale=rhs_scale, start=True, stop=True)
+
+        def weave(copy, woven, tiles):
+            copy(woven.rearrange("p (c i) t -> p c t i", i=4), tiles.rearrange("p t (c i) -> p c t i", i=4))
+
+        def quantise(words, scales, woven):
+            nc.vector.quantize_mx(out=words.bitcast(FP8X4), scales=scales, in_=woven.rearrange("p c t -> p (c t)"))
 
         xs_win = keep.tile([P, T], U8, name="xs_win")
         ds_win = keep.tile([P, G], U8, name="ds_win")
         nc.vector.memset(xs_win[:].bitcast(I32), 0)
         nc.vector.memset(ds_win[:].bitcast(I32), 0)
-
         offs_l = load_list(offs, "offs_l")
         k1_l = load_list(k1, "k1_l")
         load_scales(x_scales, xs_win)
@@ -63,48 +107,11 @@ def tile_picked_codelapminmx_none_po_kernel(tc, x_words, x_scales, d_words, d_sc
         n1_l = load_list(n1, "n1_l")
         n3_l = load_list(n3, "n3_l")
         n4_l = load_list(n4, "n4_l")
+
         g_nb = keep.tile([P, PACK], F32, name="g_nb")
         g_own = keep.tile([P, PACK], F32, name="g_own")
-        nc.scalar.activation(g_nb[:], gs_t[:], COPY, scale=0.75 * 0.0625)
-        nc.scalar.activation(g_own[:], gs_t[:], COPY, scale=-0.0625)
-
-        def deal(dealt, picked):
-            nc.vector.tensor_copy(dealt.rearrange("p (t m) -> p m t", t=PACK), picked.rearrange("p (m t) -> p m t", t=PACK))
-
-        def place_rows(plane):
-            for j in range(1, 4):
-                nc.sync.dma_start(plane[j:P:32, :].bitcast(I32), plane[8 * j:P:32, :].bitcast(I32))
-
-        def weight_words(lst, name, picked):
-            nc.vector.tensor_copy(picked[:], dw_win[:].indirect(lst[:]))
-            dealt = keep.tile([P, H], U32, name=name + "_dealt", align_bytes=64)
-            deal(dealt[:], picked[:])
-            return dealt
-
-        def product(bank, w, ws, t, rhs, rhs_scale):
-            cols = slice(P * t, P * (t + 1))
-            nc.tensor.matmul_mx(out=bank, lhsT=w[:, cols].bitcast(FP8X4), lhsT_scale=ws[:, cols],
-                                rhs=rhs.bitcast(FP8X4), rhs_scale=rhs_scale, start=True, stop=True)
-
-        halves = [slice(HALF * h, HALF * (h + 1)) for h in range(2)]
-        chunks = [slice(a, b) for a, b in zip(CHUNK_EDGES, CHUNK_EDGES[1:])]
-        last = len(chunks) - 1
-
-        def width(cols):
-            return cols.stop - cols.start
-
-        def entries(lst, cols):
-            return lst[:, cols.start // LANES:cols.stop // LANES]
-
-        def banks(name, cols, groups, tags):
-            tiles = [psum.tile([P, len(g), width(cols)], F32, name="%s_%d" % (name, b), tag=tags[b]) for b, g in enumerate(groups)]
-            return tiles, [tiles[b][:, i, :] for b, g in enumerate(groups) for i in range(len(g))]
-
-        def woven(ap):
-            return ap.rearrange("p (c i) t -> p c t i", i=4)
-
-        def planes(ap):
-            return ap.rearrange("p t (c i) -> p c t i", i=4)
+        nc.scalar.activation(g_nb[:], gs_t[:], COPY, scale=0.75 * SIXTEENTH)
+        nc.scalar.activation(g_own[:], gs_t[:], COPY, scale=-SIXTEENTH)
 
         xs_picked = keep.tile([P, S], U8, name="xs_picked")
         nc.vector.tensor_copy(xs_picked[:], xs_win[:].indirect(offs_l[:]))
@@ -114,103 +121,101 @@ def tile_picked_codelapminmx_none_po_kernel(tc, x_words, x_scales, d_words, d_sc
         w1s, xs = scales1[:, :H], scales1[:, H:]
         deal(w1s, w1s_picked[:])
         nc.vector.tensor_copy(xs.bitcast(I32), xs_picked[:].bitcast(I32))
-        place_rows(scales1)
+        place_rows(scales1, (nc.sync, nc.scalar, nc.sync))
         w1 = weight_words(k1_l, "w1", keep.tile([P, H], U32, name="w1_picked"))
         nb = [keep.tile([P, S], F32, name="nb%d" % t) for t in range(PACK)]
         h2 = [keep.tile([P, S], F32, name="h2_%d" % t) for t in range(PACK)]
-        acc1 = []
-        for h, cols in enumerate(halves):
-            xw = keep.tile([P, HALF], U32, name="xw%d" % h, align_bytes=64)
+        sums1 = []
+        for half, cols in enumerate(HALVES):
+            xw = keep.tile([P, width(cols)], U32, name="xw%d" % half, align_bytes=64)
             nc.vector.tensor_copy(xw[:], xw_win[:].indirect(entries(offs_l, cols)))
-            acc1.append(banks("acc1_%d" % h, cols, SINGLES, ["b%d" % (PACK * (1 - h) + t) for t in range(PACK)])[1])
+            sums1.append(banks("sums1_%d" % half, cols, SINGLES, FIRST_BANKS[half])[1])
             for t in range(PACK):
-                product(acc1[h][t], w1, w1s, t, xw[:], xs[:, cols])
+                product(sums1[half][t], w1, w1s, t, xw[:], xs[:, cols])
             for t in range(PACK):
-                nc.scalar.activation(nb[t][:, cols], acc1[h][t], COPY, scale=g_nb[:, t:t + 1])
+                nc.scalar.activation(nb[t][:, cols], sums1[half][t], COPY, scale=g_nb[:, t:t + 1])
 
         w2s_picked = shared.tile([P, H], U8, name="w2s_picked", offset=0)
         nc.vector.tensor_copy(w2s_picked[:], ds_win[:].indirect(k2_l[:]))
         w2s = keep.tile([P, H], U8, name="w2s", align_bytes=64)
         deal(w2s[:], w2s_picked[:])
-        place_rows(w2s)
+        place_rows(w2s, (nc.sync, nc.sync, nc.sync))
         w2 = weight_words(k2_l, "w2", shared.tile([P, H], U32, name="w2_picked", offset=H))
 
-        first = keep.tile([P, PACK, S], F32, name="first")
-        for cols in chunks:
+        at_n1 = keep.tile([P, PACK, S], F32, name="at_n1")
+        for cols in CHUNKS:
             for t in range(PACK):
-                nc.scalar.activation(first[:, t, cols], nb[t][:].indirect(entries(n1_l, cols)), COPY)
-        second = keep.tile([P, BOTH_ON_SCALAR, width(chunks[last])], F32, name="second")
-        for t in range(BOTH_ON_SCALAR):
-            nc.scalar.activation(second[:, t, :], nb[t][:].indirect(entries(n2_l, chunks[last])), COPY)
-        acc2 = []
-        bank2 = []
-        for c, cols in enumerate(chunks):
+                nc.scalar.activation(at_n1[:, t, cols], nb[t][:].indirect(entries(n1_l, cols)), COPY)
+        at_n2 = keep.tile([P, N2_ON_SCALAR, width(CHUNKS[LAST])], F32, name="at_n2")
+        for t in range(N2_ON_SCALAR):
+            nc.scalar.activation(at_n2[:, t, :], nb[t][:].indirect(entries(n2_l, CHUNKS[LAST])), COPY)
+        banks2, sums2 = [], []
+        for c, cols in enumerate(CHUNKS):
             n = width(cols)
-            h = cols.start // HALF
-            local = slice(cols.start - h * HALF, cols.stop - h * HALF)
-            parts = [slice(0, n // 2), slice(n // 2, n)] if c == last else [slice(0, n)]
+            half = cols.start // width(HALVES[0])
+            in_half = slice(cols.start - HALVES[half].start, cols.stop - HALVES[half].start)
             both = keep.tile([P, PACK, n], F32, name="both%d" % c)
-            zp = keep.tile([P, PACK, n], BF16, name="zp%d" % c)
+            z = keep.tile([P, PACK, n], BF16, name="z%d" % c)
             for t in range(PACK + 1):
-                if c == last and t < BOTH_ON_SCALAR:
+                if c == LAST and t < N2_ON_SCALAR:
                     if t == 0:
-                        nc.vector.tensor_tensor(both[:, :BOTH_ON_SCALAR, :], second[:], first[:, :BOTH_ON_SCALAR, cols], ALU.add)
+                        nc.vector.tensor_tensor(both[:, :N2_ON_SCALAR, :], at_n2[:], at_n1[:, :N2_ON_SCALAR, cols], ALU.add)
                 elif t < PACK:
-                    nc.vector.tensor_tensor(both[:, t, :], nb[t][:].indirect(entries(n2_l, cols)), first[:, t, cols], ALU.add)
+                    nc.vector.tensor_tensor(both[:, t, :], nb[t][:].indirect(entries(n2_l, cols)), at_n1[:, t, cols], ALU.add)
                 if t > 0:
-                    for part in parts if t == PACK else [slice(0, n)]:
-                        nc.vector.scalar_tensor_tensor(zp[:, t - 1, part], acc1[h][t - 1][:, local][:, part], g_own[:, t - 1:t],
-                                                       both[:, t - 1, part], ALU.mult, ALU.add)
-            z = keep.tile([P, n, PACK], BF16, name="z%d" % c, align_bytes=64)
-            weave = nc.scalar.copy if c < last else nc.vector.tensor_copy
+                    for piece in pieces(c) if t == PACK else [slice(0, n)]:
+                        nc.vector.scalar_tensor_tensor(z[:, t - 1, piece], sums1[half][t - 1][:, in_half][:, piece],
+                                                       g_own[:, t - 1:t], both[:, t - 1, piece], ALU.mult, ALU.add)
+            z_woven = keep.tile([P, n, PACK], BF16, name="z_woven%d" % c, align_bytes=64)
             zw = keep.tile([P, n], U32, name="zw%d" % c, align_bytes=64)
             zs = keep.tile([P, n], U8, name="zs%d" % c, align_bytes=64)
-            for part in parts:
-                weave(woven(z[:, part, :]), planes(zp[:, :, part]))
-            for part in parts:
-                nc.vector.quantize_mx(out=zw[:, part].bitcast(FP8X4), scales=zs[:, part], in_=z[:, part, :].rearrange("p c t -> p (c t)"))
-            tiles, sums = banks("acc2_%d" % c, cols, GROUPS[c], TAGS[c])
-            bank2.append(tiles)
-            acc2.append(sums)
+            for piece in pieces(c):
+                weave(nc.vector.tensor_copy if c == LAST else nc.scalar.copy, z_woven[:, piece, :], z[:, :, piece])
+            for piece in pieces(c):
+                quantise(zw[:, piece], zs[:, piece], z_woven[:, piece, :])
+            tiles, sums = banks("sums2_%d" % c, cols, BANK_GROUPS[c], SECOND_BANKS[c])
+            banks2.append(tiles)
+            sums2.append(sums)
             for t in range(PACK):
-                product(acc2[c][t], w2, w2s, t, zw[:], zs[:])
-        for c in range(len(chunks)):
+                product(sums2[c][t], w2, w2s, t, zw[:], zs[:])
+
+        for c, cols in enumerate(CHUNKS):
             for t in range(PACK):
-                nc.scalar.activation(h2[t][:, chunks[c]], acc2[c][t], COPY, scale=0.0625)
+                if c == LAST:
+                    nc.vector.tensor_scalar_mul(h2[t][:, cols], sums2[c][t], SIXTEENTH)
+                else:
+                    nc.scalar.activation(h2[t][:, cols], sums2[c][t], COPY, scale=SIXTEENTH)
 
         out_rows = out_0.rearrange("(p t) s -> p t s", t=PACK)
-        words_out = out_1[0].rearrange("p n t -> p (n t)").bitcast(I32)
+        out_words = out_1[0].rearrange("p n t -> p (n t)").bitcast(I32)
         ys = keep.tile([P, S], U8, name="ys", align_bytes=64)
-        for c, cols in enumerate(chunks):
+        for c, cols in enumerate(CHUNKS):
             n = width(cols)
             y = keep.tile([P, PACK, n], F32, name="y%d" % c)
-            third = keep.tile([P, PACK, n], F32, name="third%d" % c)
-            fourth = keep.tile([P, PACK, n], F32, name="fourth%d" % c)
-            upper = keep.tile([P, PACK, n], F32, name="upper%d" % c)
+            at_n3 = keep.tile([P, PACK, n], F32, name="at_n3_%d" % c)
+            at_n4 = keep.tile([P, PACK, n], F32, name="at_n4_%d" % c)
+            larger = keep.tile([P, PACK, n], F32, name="larger%d" % c)
+            for t in range(N4_ON_VECTOR[c]):
+                nc.vector.tensor_copy(at_n4[:, t, :], h2[t][:].indirect(entries(n4_l, cols)))
             for t in range(PACK):
-                if t < ON_VECTOR[c]:
-                    nc.vector.tensor_copy(fourth[:, t, :], h2[t][:].indirect(entries(n4_l, cols)))
-            for t in range(PACK):
-                nc.scalar.activation(third[:, t, :], h2[t][:].indirect(entries(n3_l, cols)), COPY)
-            for t in range(PACK):
-                if t >= ON_VECTOR[c]:
-                    nc.scalar.activation(fourth[:, t, :], h2[t][:].indirect(entries(n4_l, cols)), COPY)
-            for bank, group in zip(bank2[c], GROUPS[c]):
+                nc.scalar.activation(at_n3[:, t, :], h2[t][:].indirect(entries(n3_l, cols)), COPY)
+            for t in range(N4_ON_VECTOR[c], PACK):
+                nc.scalar.activation(at_n4[:, t, :], h2[t][:].indirect(entries(n4_l, cols)), COPY)
+            for bank, group in zip(banks2[c], BANK_GROUPS[c]):
                 rows = slice(group.start, group.stop)
-                nc.vector.scalar_tensor_tensor(upper[:, rows, :], bank[:], 0.0625, third[:, rows, :], ALU.mult, ALU.max)
-            parts = [slice(0, n // 2), slice(n // 2, n)] if c == last else [slice(0, n)]
-            split = 3 if c == last else 2
-            nc.vector.tensor_tensor(y[:, :split, :], upper[:, :split, :], fourth[:, :split, :], ALU.min)
-            for part in parts:
-                nc.vector.tensor_tensor(y[:, split:, part], upper[:, split:, part], fourth[:, split:, part], ALU.min)
+                nc.vector.scalar_tensor_tensor(larger[:, rows, :], bank[:], SIXTEENTH, at_n3[:, rows, :], ALU.mult, ALU.max)
+            early = PACK - 1 if c == LAST else PACK // 2
+            nc.vector.tensor_tensor(y[:, :early, :], larger[:, :early, :], at_n4[:, :early, :], ALU.min)
+            for piece in pieces(c):
+                nc.vector.tensor_tensor(y[:, early:, piece], larger[:, early:, piece], at_n4[:, early:, piece], ALU.min)
             nc.sync.dma_start(out_rows[:, :, cols], y[:])
-            yb = keep.tile([P, n, PACK], BF16, name="yb%d" % c, align_bytes=64)
+            y_woven = keep.tile([P, n, PACK], BF16, name="y_woven%d" % c, align_bytes=64)
             yw = keep.tile([P, n], U32, name="yw%d" % c, align_bytes=64)
-            for part in parts:
-                nc.vector.tensor_copy(woven(yb[:, part, :]), planes(y[:, :, part]))
-            for part in parts:
-                nc.vector.quantize_mx(out=yw[:, part].bitcast(FP8X4), scales=ys[:, cols][:, part], in_=yb[:, part, :].rearrange("p c t -> p (c t)"))
-            nc.sync.dma_start(words_out[:, cols], yw[:].bitcast(I32))
-        for q in range(4):
+            for piece in pieces(c):
+                weave(nc.vector.tensor_copy, y_woven[:, piece, :], y[:, :, piece])
+            for piece in pieces(c):
+                quantise(yw[:, piece], ys[:, cols][:, piece], y_woven[:, piece, :])
+            nc.sync.dma_start(out_words[:, cols], yw[:].bitcast(I32))
+        for q in range(P // QUADRANT):
             queue = nc.sync if q % 2 == 0 else nc.scalar
-            queue.dma_start(out_2[0, 4 * q:4 * q + 4, :].bitcast(I32), ys[32 * q:32 * q + 4, :].bitcast(I32))
+            queue.dma_start(out_2[0, PACK * q:PACK * (q + 1), :].bitcast(I32), ys[QUADRANT * q:QUADRANT * q + PACK, :].bitcast(I32))

from contextlib import ExitStack

import concourse.mybir as mybir

K, T, S, G, H = 512, 1024, 512, 2048, 512
FLOPS = 2 * 2 * K * H * S

F32 = mybir.dt.float32
BF16 = mybir.dt.bfloat16
I32 = mybir.dt.int32
U32 = mybir.dt.uint32
U16 = mybir.dt.uint16
U8 = mybir.dt.uint8
FP8X4 = mybir.dt.float8_e4m3fn_x4
ALU = mybir.AluOpType
COPY = mybir.ActivationFunctionType.Copy

P = 128
PACK = 4
LANES = 16
QUADRANT = 32
BLOCK_PARTITIONS = 8
SIXTEENTH = 0.0625

HALVES = (slice(0, 256), slice(256, 512))
CHUNKS = (slice(0, 256), slice(256, 384), slice(384, 512))
LAST = len(CHUNKS) - 1
SINGLES = (range(0, 1), range(1, 2), range(2, 3), range(3, 4))
BANK_GROUPS = ((range(0, 2), range(2, 4)), (range(0, 4),), (range(0, 1), range(1, 4)))
FIRST_BANKS = (("b4", "b5", "b6", "b7"), ("b0", "b1", "b2", "b3"))
SECOND_BANKS = (("b4", "b5"), ("b6",), ("b7", "b0"))
N2_ON_SCALAR = 2
N4_ON_VECTOR = (4, 1, 0)


def tile_picked_codelapminmx_none_po_kernel(
    tc, x_words, x_scales, d_words, d_scales, gs, offs, k1, n1, n2, k2, n3, n4, out_0, out_1, out_2
):
    nc = tc.nc
    with ExitStack() as ctx:
        keep = ctx.enter_context(tc.tile_pool(name="keep", bufs=1))
        shared = ctx.enter_context(tc.tile_pool(name="shared", bufs=1))
        psum = ctx.enter_context(tc.psum_pool(name="psum", bufs=1))

        def width(cols):
            return cols.stop - cols.start

        def entries(lst, cols):
            return lst[:, cols.start // LANES:cols.stop // LANES]

        def pieces(c):
            n = width(CHUNKS[c])
            return [slice(0, n // 2), slice(n // 2, n)] if c == LAST else [slice(0, n)]

        def load_list(src, name):
            lst = keep.tile([P, S // LANES], U16, name=name)
            nc.sync.dma_start(lst[:], src)
            return lst

        def load_scales(src, win):
            nc.sync.dma_start(win[0:P:BLOCK_PARTITIONS, :].bitcast(I32), src[0].bitcast(I32))

        def deal(dealt, picked):
            nc.vector.tensor_copy(dealt.rearrange("p (t m) -> p m t", t=PACK), picked.rearrange("p (m t) -> p m t", t=PACK))

        def place_rows(scales, queues):
            for j, queue in zip(range(1, PACK), queues):
                queue.dma_start(scales[j:P:QUADRANT, :].bitcast(I32), scales[BLOCK_PARTITIONS * j:P:QUADRANT, :].bitcast(I32))

        def weight_words(lst, name, picked):
            nc.vector.tensor_copy(picked[:], dw_win[:].indirect(lst[:]))
            dealt = keep.tile([P, H], U32, name=name, align_bytes=64)
            deal(dealt[:], picked[:])
            return dealt

        def banks(name, cols, groups, tags):
            tiles = [psum.tile([P, len(g), width(cols)], F32, name="%s_%d" % (name, b), tag=tags[b]) for b, g in enumerate(groups)]
            return tiles, [tiles[b][:, i, :] for b, g in enumerate(groups) for i in range(len(g))]

        def product(sums, w, ws, t, rhs, rhs_scale):
            cols = slice(P * t, P * (t + 1))
            nc.tensor.matmul_mx(out=sums, lhsT=w[:, cols].bitcast(FP8X4), lhsT_scale=ws[:, cols],
                                rhs=rhs.bitcast(FP8X4), rhs_scale=rhs_scale, start=True, stop=True)

        def weave(copy, woven, tiles):
            copy(woven.rearrange("p (c i) t -> p c t i", i=4), tiles.rearrange("p t (c i) -> p c t i", i=4))

        def quantise(words, scales, woven):
            nc.vector.quantize_mx(out=words.bitcast(FP8X4), scales=scales, in_=woven.rearrange("p c t -> p (c t)"))

        xs_win = keep.tile([P, T], U8, name="xs_win")
        ds_win = keep.tile([P, G], U8, name="ds_win")
        nc.vector.memset(xs_win[:].bitcast(I32), 0)
        nc.vector.memset(ds_win[:].bitcast(I32), 0)
        offs_l = load_list(offs, "offs_l")
        k1_l = load_list(k1, "k1_l")
        load_scales(x_scales, xs_win)
        load_scales(d_scales, ds_win)
        gs_t = keep.tile([P, PACK], F32, name="gs_t")
        nc.sync.dma_start(gs_t[:], gs.rearrange("(p t) o -> p (t o)", t=PACK))
        k2_l = load_list(k2, "k2_l")
        dw_win = keep.tile([P, G], U32, name="dw_win")
        nc.sync.dma_start(dw_win[:].bitcast(I32), d_words[0].rearrange("p n t -> p (n t)").bitcast(I32))
        xw_win = shared.tile([P, T], U32, name="xw_win", offset=0)
        nc.sync.dma_start(xw_win[:].bitcast(I32), x_words[0].rearrange("p n t -> p (n t)").bitcast(I32))
        n2_l = load_list(n2, "n2_l")
        n1_l = load_list(n1, "n1_l")
        n3_l = load_list(n3, "n3_l")
        n4_l = load_list(n4, "n4_l")

        g_nb = keep.tile([P, PACK], F32, name="g_nb")
        g_own = keep.tile([P, PACK], F32, name="g_own")
        nc.scalar.activation(g_nb[:], gs_t[:], COPY, scale=0.75 * SIXTEENTH)
        nc.scalar.activation(g_own[:], gs_t[:], COPY, scale=-SIXTEENTH)

        xs_picked = keep.tile([P, S], U8, name="xs_picked")
        nc.vector.tensor_copy(xs_picked[:], xs_win[:].indirect(offs_l[:]))
        w1s_picked = keep.tile([P, H], U8, name="w1s_picked")
        nc.vector.tensor_copy(w1s_picked[:], ds_win[:].indirect(k1_l[:]))
        scales1 = keep.tile([P, H + S], U8, name="scales1", align_bytes=64)
        w1s, xs = scales1[:, :H], scales1[:, H:]
        deal(w1s, w1s_picked[:])
        nc.vector.tensor_copy(xs.bitcast(I32), xs_picked[:].bitcast(I32))
        place_rows(scales1, (nc.sync, nc.scalar, nc.sync))
        w1 = weight_words(k1_l, "w1", keep.tile([P, H], U32, name="w1_picked"))
        nb = [keep.tile([P, S], F32, name="nb%d" % t) for t in range(PACK)]
        h2 = [keep.tile([P, S], F32, name="h2_%d" % t) for t in range(PACK)]
        sums1 = []
        for half, cols in enumerate(HALVES):
            xw = keep.tile([P, width(cols)], U32, name="xw%d" % half, align_bytes=64)
            nc.vector.tensor_copy(xw[:], xw_win[:].indirect(entries(offs_l, cols)))
            sums1.append(banks("sums1_%d" % half, cols, SINGLES, FIRST_BANKS[half])[1])
            for t in range(PACK):
                product(sums1[half][t], w1, w1s, t, xw[:], xs[:, cols])
            for t in range(PACK):
                nc.scalar.activation(nb[t][:, cols], sums1[half][t], COPY, scale=g_nb[:, t:t + 1])

        w2s_picked = shared.tile([P, H], U8, name="w2s_picked", offset=0)
        nc.vector.tensor_copy(w2s_picked[:], ds_win[:].indirect(k2_l[:]))
        w2s = keep.tile([P, H], U8, name="w2s", align_bytes=64)
        deal(w2s[:], w2s_picked[:])
        place_rows(w2s, (nc.sync, nc.sync, nc.sync))
        w2 = weight_words(k2_l, "w2", shared.tile([P, H], U32, name="w2_picked", offset=H))

        at_n1 = keep.tile([P, PACK, S], F32, name="at_n1")
        for cols in CHUNKS:
            for t in range(PACK):
                nc.scalar.activation(at_n1[:, t, cols], nb[t][:].indirect(entries(n1_l, cols)), COPY)
        at_n2 = keep.tile([P, N2_ON_SCALAR, width(CHUNKS[LAST])], F32, name="at_n2")
        for t in range(N2_ON_SCALAR):
            nc.scalar.activation(at_n2[:, t, :], nb[t][:].indirect(entries(n2_l, CHUNKS[LAST])), COPY)
        banks2, sums2 = [], []
        for c, cols in enumerate(CHUNKS):
            n = width(cols)
            half = cols.start // width(HALVES[0])
            in_half = slice(cols.start - HALVES[half].start, cols.stop - HALVES[half].start)
            both = keep.tile([P, PACK, n], F32, name="both%d" % c)
            z = keep.tile([P, PACK, n], BF16, name="z%d" % c)
            for t in range(PACK + 1):
                if c == LAST and t < N2_ON_SCALAR:
                    if t == 0:
                        nc.vector.tensor_tensor(both[:, :N2_ON_SCALAR, :], at_n2[:], at_n1[:, :N2_ON_SCALAR, cols], ALU.add)
                elif t < PACK:
                    nc.vector.tensor_tensor(both[:, t, :], nb[t][:].indirect(entries(n2_l, cols)), at_n1[:, t, cols], ALU.add)
                if t > 0:
                    for piece in pieces(c) if t == PACK else [slice(0, n)]:
                        nc.vector.scalar_tensor_tensor(z[:, t - 1, piece], sums1[half][t - 1][:, in_half][:, piece],
                                                       g_own[:, t - 1:t], both[:, t - 1, piece], ALU.mult, ALU.add)
            z_woven = keep.tile([P, n, PACK], BF16, name="z_woven%d" % c, align_bytes=64)
            zw = keep.tile([P, n], U32, name="zw%d" % c, align_bytes=64)
            zs = keep.tile([P, n], U8, name="zs%d" % c, align_bytes=64)
            for piece in pieces(c):
                weave(nc.vector.tensor_copy if c == LAST else nc.scalar.copy, z_woven[:, piece, :], z[:, :, piece])
            for piece in pieces(c):
                quantise(zw[:, piece], zs[:, piece], z_woven[:, piece, :])
            tiles, sums = banks("sums2_%d" % c, cols, BANK_GROUPS[c], SECOND_BANKS[c])
            banks2.append(tiles)
            sums2.append(sums)
            for t in range(PACK):
                product(sums2[c][t], w2, w2s, t, zw[:], zs[:])

        for c, cols in enumerate(CHUNKS):
            for t in range(PACK):
                if c == LAST:
                    nc.vector.tensor_scalar_mul(h2[t][:, cols], sums2[c][t], SIXTEENTH)
                else:
                    nc.scalar.activation(h2[t][:, cols], sums2[c][t], COPY, scale=SIXTEENTH)

        out_rows = out_0.rearrange("(p t) s -> p t s", t=PACK)
        out_words = out_1[0].rearrange("p n t -> p (n t)").bitcast(I32)
        ys = keep.tile([P, S], U8, name="ys", align_bytes=64)
        for c, cols in enumerate(CHUNKS):
            n = width(cols)
            y = keep.tile([P, PACK, n], F32, name="y%d" % c)
            at_n3 = keep.tile([P, PACK, n], F32, name="at_n3_%d" % c)
            at_n4 = keep.tile([P, PACK, n], F32, name="at_n4_%d" % c)
            larger = keep.tile([P, PACK, n], F32, name="larger%d" % c)
            for t in range(N4_ON_VECTOR[c]):
                nc.vector.tensor_copy(at_n4[:, t, :], h2[t][:].indirect(entries(n4_l, cols)))
            for t in range(PACK):
                nc.scalar.activation(at_n3[:, t, :], h2[t][:].indirect(entries(n3_l, cols)), COPY)
            for t in range(N4_ON_VECTOR[c], PACK):
                nc.scalar.activation(at_n4[:, t, :], h2[t][:].indirect(entries(n4_l, cols)), COPY)
            for bank, group in zip(banks2[c], BANK_GROUPS[c]):
                rows = slice(group.start, group.stop)
                nc.vector.scalar_tensor_tensor(larger[:, rows, :], bank[:], SIXTEENTH, at_n3[:, rows, :], ALU.mult, ALU.max)
            early = PACK - 1 if c == LAST else PACK // 2
            nc.vector.tensor_tensor(y[:, :early, :], larger[:, :early, :], at_n4[:, :early, :], ALU.min)
            for piece in pieces(c):
                nc.vector.tensor_tensor(y[:, early:, piece], larger[:, early:, piece], at_n4[:, early:, piece], ALU.min)
            nc.sync.dma_start(out_rows[:, :, cols], y[:])
            y_woven = keep.tile([P, n, PACK], BF16, name="y_woven%d" % c, align_bytes=64)
            yw = keep.tile([P, n], U32, name="yw%d" % c, align_bytes=64)
            for piece in pieces(c):
                weave(nc.vector.tensor_copy, y_woven[:, piece, :], y[:, :, piece])
            for piece in pieces(c):
                quantise(yw[:, piece], ys[:, cols][:, piece], y_woven[:, piece, :])
            nc.sync.dma_start(out_words[:, cols], yw[:].bitcast(I32))
        for q in range(P // QUADRANT):
            queue = nc.sync if q % 2 == 0 else nc.scalar
            queue.dma_start(out_2[0, PACK * q:PACK * (q + 1), :].bitcast(I32), ys[QUADRANT * q:QUADRANT * q + PACK, :].bitcast(I32))
